import numpy as np
import ml_dtypes


def mxq(x, axis, fmt="e4m3"):
    dtype, down = {"e4m3": (ml_dtypes.float8_e4m3fn, 7), "e5m2": (ml_dtypes.float8_e5m2, 14)}[fmt]
    v = np.moveaxis(np.asarray(x, np.float32).astype(ml_dtypes.bfloat16).astype(np.float64), axis, -1)
    blocks = v.reshape(v.shape[:-1] + (-1, 32))
    amax = np.abs(blocks).max(-1, keepdims=True)
    byte = np.maximum(np.where(amax > 0, np.frexp(amax)[1] - 1 + 127, 0) - down, 1)
    scale = np.exp2(byte - 127.0)
    codes = (blocks / scale).astype(np.float32).astype(dtype).astype(np.float64)
    return np.moveaxis((codes * scale).reshape(v.shape), -1, axis)


WIDE = False


def mx_kscale(k):
    if not WIDE:
        return np.ones(k)
    levels = np.array([10, -10, 5, -5, 0])
    if k % 512:
        return np.exp2(np.random.permutation(np.resize(levels, k // 32))).repeat(32)
    a = np.empty((k // 512, 16))
    for p in range(k // 512):
        a[p, :8] = np.random.permutation(np.resize(levels, 8))
        for g in range(8):
            far = levels[np.abs(levels - a[p, g]) >= 10]
            a[p, g + 8] = far[np.random.randint(len(far))]
    return np.exp2(a.ravel()).repeat(32)


def f64(x):
    return np.asarray(x).astype(np.float64)


def striped(idx):
    return np.tile(np.asarray(idx).reshape(-1, 16).T, (8, 1)).astype(np.uint16)


def unstriped(offs):
    return offs[:16].T.reshape(-1).astype(np.int64)


def striped8(idx):
    return np.asarray(idx).reshape(8, -1, 16).transpose(0, 2, 1).reshape(128, -1).astype(np.uint16)


def unstriped8(offs):
    return offs.reshape(8, 16, -1).transpose(0, 2, 1).reshape(8, -1).astype(np.int64)


def pick8(x, idx, run):
    r = np.arange(len(x))
    return x[r[:, None], idx[r % (8 * run) // run]]


E2M1 = np.array([0.0, 0.5, 1.0, 1.5, 2.0, 3.0, 4.0, 6.0, -0.0, -0.5, -1.0, -1.5, -2.0, -3.0, -4.0, -6.0])


def pack_weight(w, fmt):
    k, n = w.shape
    w = f64(np.asarray(w, np.float32).astype(ml_dtypes.bfloat16)).reshape(k // 32, 32, n)
    amax = np.abs(w).max(1)
    if fmt == "e4m3":
        byte = np.frexp(amax)[1] - 1 + 127 - 7
    else:
        mant, ex = np.frexp(amax / 6.0)
        byte = np.where(mant > 0.5, ex, ex - 1) + 127
    byte = np.clip(np.where(amax > 0, byte, 1), 1, 254)
    scaled = (w * np.exp2(127.0 - byte)[:, None, :]).reshape(k, n).astype(np.float32)
    by_word = np.ascontiguousarray(scaled.reshape(k // 512, 128, 4, n).transpose(0, 1, 3, 2))
    if fmt == "e4m3":
        words = by_word.astype(ml_dtypes.float8_e4m3fn).view(np.uint8)
    else:
        c = by_word.astype(ml_dtypes.float4_e2m1fn).view(np.uint8) & 0xF
        words = (c[..., 0::2] | (c[..., 1::2] << 4)).reshape(k // 512, 128, 2 * n)
    return np.ascontiguousarray(words), np.ascontiguousarray(byte.astype(np.uint8).reshape(k // 512, 16, n))


def unpack_weight(words, scales, fmt):
    g, _, n = scales.shape
    words = np.ascontiguousarray(words).reshape(g, 128, n, -1)
    if fmt == "e4m3":
        vals = words.view(ml_dtypes.float8_e4m3fn).astype(np.float64)
    else:
        nib = np.empty((g, 128, n, 4), np.uint8)
        nib[..., 0::2] = words & 0xF
        nib[..., 1::2] = words >> 4
        vals = E2M1[nib]
    vals = vals * np.repeat(np.exp2(scales.astype(np.float64) - 127.0), 8, axis=1)[..., None]
    return vals.transpose(0, 1, 3, 2).reshape(g * 512, n)


def sigmoid(v):
    return 1.0 / (1.0 + np.exp(-v))


K, R, F, T, J, M, G = 512, 128, 512, 2048, 512, 256, 32


def setup_inputs():
    n = np.random.standard_normal
    idx = np.random.permutation(T)[:J]
    idx2 = np.stack([np.random.permutation(J)[:M] for _ in range(8)])
    fk = mx_kscale(K)
    ff = mx_kscale(F)
    tabp = pack_weight(n((K, T)) / fk[:, None], "e4m3")
    dtabp = pack_weight(n((K, T)) / fk[:, None], "e4m3")
    return {
        "tab_words": tabp[0],
        "tab_scales": tabp[1],
        "w1": (n((K, R)) * 1 / np.sqrt(K) * fk[:, None]).astype(np.float32),
        "gain": (np.random.uniform(0.5, 1.5, (R, 1))).astype(np.float32),
        "share": (np.random.uniform(0.4, 1.0, (R, 1))).astype(np.float32),
        "pb": (np.random.uniform(-0.5, 0.5, (1, M))).astype(np.float32),
        "wo": (n((F, R)) * 1 / np.sqrt(F) * ff[:, None]).astype(np.float32),
        "dy": (n((F, M)) / ff[:, None]).astype(np.float32),
        "dtab_words": dtabp[0],
        "dtab_scales": dtabp[1],
        "og": (np.random.uniform(0.7, 2.0, (R, 1))).astype(np.float32),
        "base": (0.3 * n((R, J))).astype(np.float32),
        "offs": striped(idx),
        "offs2": striped8(idx2),
    }


def reference(tab_words, tab_scales, w1, gain, share, pb, wo, dy, dtab_words, dtab_scales, og, base, offs, offs2):
    idx = unstriped(offs)
    idx2 = unstriped8(offs2)
    tabu = unpack_weight(tab_words, tab_scales, "e4m3")
    dtabu = unpack_weight(dtab_words, dtab_scales, "e4m3")
    w1q = mxq(f64(w1), 0, "e4m3")
    tabidxg = tabu[:, idx]
    a = w1q.T @ tabidxg
    dtabidxg = dtabu[:, idx]
    ta = w1q.T @ dtabidxg
    h0 = np.tanh(a)
    h1 = h0 * f64(gain)
    s = pick8(h1, idx2, 16) + f64(pb)
    m1 = s.reshape(R, G, M // G).mean(axis=2)
    mr = np.repeat(m1, M // G, axis=1)
    woq = mxq(f64(wo), 0, "e4m3")
    dyq = mxq(f64(dy), 0, "e4m3")
    c0 = woq.T @ dyq
    dmr = c0 * sigmoid(s - mr * f64(share)) * (-1.0) * f64(share)
    dm1 = dmr.reshape(R, G, M // G).sum(axis=2)
    e1 = dm1 / 8.0
    r1 = np.repeat(e1, M // G, axis=1)
    ds = c0 * sigmoid(s - mr * f64(share)) + r1
    s2 = np.zeros((R, J))
    s2[np.arange(R)[:, None], idx2[np.arange(R) % 128 // 16]] = ds
    dh0 = s2 * f64(gain)
    xh0 = ta * (1.0 - np.square(h0))
    xh1 = xh0 * f64(gain)
    xs = pick8(xh1, idx2, 16)
    xm1 = xs.reshape(R, G, M // G).mean(axis=2)
    xmr = np.repeat(xm1, M // G, axis=1)
    xdmr = (xs - xmr * f64(share)) * sigmoid(s - mr * f64(share)) * (1.0 - sigmoid(s - mr * f64(share))) * c0 * (-1.0) * f64(share)
    xdm1 = xdmr.reshape(R, G, M // G).sum(axis=2)
    xe1 = xdm1 / 8.0
    xr1 = np.repeat(xe1, M // G, axis=1)
    xds = (xs - xmr * f64(share)) * sigmoid(s - mr * f64(share)) * (1.0 - sigmoid(s - mr * f64(share))) * c0 + xr1
    xs2 = np.zeros((R, J))
    xs2[np.arange(R)[:, None], idx2[np.arange(R) % 128 // 16]] = xds
    xdh0 = xs2 * f64(gain)
    xda = xdh0 * (1.0 - np.square(h0)) + xh0 * h0 * 2.0 * (-1.0) * dh0
    y = xda * f64(og) + f64(base)
    return y

@@ -1,0 +1,233 @@
+from contextlib import ExitStack
+
+import concourse.mybir as mybir
+from concourse.masks import make_identity
+
+K, R, F, T, J, M, G = 512, 128, 512, 2048, 512, 256, 32
+FLOPS = 2 * K * R * J * 2 + 2 * F * R * M
+
+F32 = mybir.dt.float32
+BF16 = mybir.dt.bfloat16
+I32 = mybir.dt.int32
+U32 = mybir.dt.uint32
+U16 = mybir.dt.uint16
+U8 = mybir.dt.uint8
+FP8X4 = mybir.dt.float8_e4m3fn_x4
+ALU = mybir.AluOpType
+ACT = mybir.ActivationFunctionType
+AX = mybir.AxisListType
+
+P = 128
+PACK = 4
+GROUP = M // G
+HALF = J // 2
+LIST_HALF = HALF // 16
+DTAB_ROW = 4
+TINY = 1e-30
+
+
+def tile_attend_hvcpickcentred_kernel(
+    tc, tab_words, tab_scales, w1, gain, share, pb, wo, dy, dtab_words, dtab_scales, og, base, offs, offs2, out
+):
+    nc = tc.nc
+    with ExitStack() as ctx:
+        sb = ctx.enter_context(tc.tile_pool(name="sb", bufs=1))
+        ps = ctx.enter_context(tc.psum_pool(name="ps", bufs=1))
+
+        def grouped(t):
+            return t.rearrange("p (g e) -> p g e", e=GROUP)
+
+        def group_sum(name, x):
+            total = sb.tile([P, G], F32, name=name)
+            nc.vector.tensor_reduce(out=total[:], in_=grouped(x[:]), axis=AX.X, op=ALU.add)
+            return total
+
+        def centre(name, x, total, neg_k):
+            res = sb.tile([P, M], F32, name=name)
+            nc.vector.scalar_tensor_tensor(
+                out=grouped(res[:]),
+                in0=total[:].unsqueeze(2).to_broadcast([P, G, GROUP]),
+                scalar=neg_k[:],
+                in1=grouped(x[:]),
+                op0=ALU.mult,
+                op1=ALU.add,
+            )
+            return res
+
+        offs_t = sb.tile([P, J // 16], U16, name="offs_t")
+        offs2_t = sb.tile([P, M // 16], U16, name="offs2_t")
+        tab_w = sb.tile([P, T], U32, name="tab_w", tag="tab_then_dtab_gs", align_bytes=64)
+        dtab_w = sb.tile([P, T], U32, name="dtab_w", tag="dtab_then_base", align_bytes=64)
+        tab_s = sb.tile([P, T], U8, name="tab_s", tag="tab_scales_then_picked", align_bytes=64)
+        dtab_s = sb.tile([P, T], U8, name="dtab_s", tag="dtab_scales_then_picked", align_bytes=64)
+        w1_raw = sb.tile([P, PACK, R], F32, name="w1_raw", tag="weights_raw")
+        gain_t = sb.tile([P, 1], F32, name="gain_t")
+        share_t = sb.tile([P, 1], F32, name="share_t")
+        og_t = sb.tile([P, 1], F32, name="og_t")
+        pb_t = sb.tile([P, 2], F32, name="pb_t")
+        placed = sb.tile([P, J], F32, name="placed")
+        ident = sb.tile([P, P], F32, name="ident")
+
+        nc.vector.memset(dtab_s[:].bitcast(I32), 0)
+        nc.vector.memset(tab_s[:].bitcast(I32), 0)
+        nc.vector.memset(placed[:], 0.0)
+
+        nc.sync.dma_start(offs_t[:], offs)
+        nc.scalar.dma_start(out=gain_t[:], in_=gain)
+        nc.sync.dma_start(offs2_t[:], offs2)
+        nc.scalar.dma_start(out=pb_t[:], in_=pb.rearrange("o (p c) -> (o p) c", c=2))
+        nc.sync.dma_start(out=w1_raw[:], in_=w1.rearrange("(p j) r -> p j r", j=PACK))
+        nc.scalar.dma_start(out=share_t[:], in_=share)
+        nc.sync.dma_start(out=tab_w[:].bitcast(I32), in_=tab_words[0].rearrange("p n t -> p (n t)").bitcast(I32))
+        nc.scalar.dma_start(out=og_t[:], in_=og)
+        nc.sync.dma_start(out=dtab_w[:].bitcast(I32), in_=dtab_words[0].rearrange("p n t -> p (n t)").bitcast(I32))
+        for i in range(4):
+            nc.scalar.dma_start(out=tab_s[i:P:32, :].bitcast(I32), in_=tab_scales[0, i:16:4, :].bitcast(I32))
+        make_identity(nc, ident[:])
+        for i in range(4):
+            nc.gpsimd.dma_start(
+                out=dtab_s[DTAB_ROW + i : P : 32, :].bitcast(I32), in_=dtab_scales[0, i:16:4, :].bitcast(I32)
+            )
+
+        neg_gain = sb.tile([P, 1], F32, name="neg_gain")
+        neg_k = sb.tile([P, 1], F32, name="neg_k")
+        is_tiny = sb.tile([P, 1], F32, name="is_tiny")
+        safe_gain = sb.tile([P, 1], F32, name="safe_gain")
+        inv_gain = sb.tile([P, 1], F32, name="inv_gain")
+        q_fac = sb.tile([P, 1], F32, name="q_fac")
+        b_fac = sb.tile([P, 1], F32, name="b_fac")
+        nc.vector.tensor_scalar(neg_gain[:], gain_t[:], -1.0, 0.0, ALU.mult, ALU.add)
+        nc.vector.tensor_scalar(is_tiny[:], gain_t[:], gain_t[:], TINY, ALU.mult, ALU.is_lt)
+        nc.vector.tensor_scalar(safe_gain[:], gain_t[:], is_tiny[:], 1.0, ALU.add, ALU.mult)
+        nc.vector.reciprocal(inv_gain[:], safe_gain[:])
+        nc.vector.tensor_scalar(neg_k[:], share_t[:], -1.0 / GROUP, 0.0, ALU.mult, ALU.add)
+        nc.vector.tensor_scalar(q_fac[:], og_t[:], gain_t[:], 0.25, ALU.mult, ALU.mult)
+        nc.vector.tensor_scalar(b_fac[:], og_t[:], inv_gain[:], -1.0, ALU.mult, ALU.mult)
+
+        def interleave(name, raw, width, tag):
+            inter = sb.tile([P, width, PACK], BF16, name=name, tag=tag, align_bytes=64)
+            nc.scalar.activation(out=inter[:], in_=raw[:].rearrange("p j w -> p w j"), func=ACT.Copy)
+            return inter
+
+        def quantise(name, inter, width):
+            codes = sb.tile([P, width], U32, name=name + "_codes", align_bytes=64)
+            scales = sb.tile([P, width], U8, name=name + "_scales", align_bytes=64)
+            nc.vector.quantize_mx(
+                out=codes[:].bitcast(FP8X4), scales=scales[:], in_=inter[:].rearrange("p w j -> p (w j)")
+            )
+            return codes, scales
+
+        w1_inter = interleave("w1_inter", w1_raw, R, "w1_inter_then_dy")
+        wo_raw = sb.tile([P, PACK, R], F32, name="wo_raw", tag="weights_raw")
+        nc.sync.dma_start(out=wo_raw[:], in_=wo.rearrange("(p j) r -> p j r", j=PACK))
+        tab_gs = sb.tile([P, J], U8, name="tab_gs", align_bytes=64)
+        nc.vector.tensor_copy(tab_gs[:], tab_s[:].indirect(offs_t[:]))
+        w1_codes, w1_scales = quantise("w1", w1_inter, R)
+        dy_raw = sb.tile([P, PACK, M], F32, name="dy_raw", tag="w1_inter_then_dy", align_bytes=64)
+        nc.sync.dma_start(out=dy_raw[:], in_=dy.rearrange("(p j) m -> p j m", j=PACK))
+
+        pb_ps = ps.tile([P, 2, P], F32, name="pb_ps")
+        for c in range(2):
+            nc.tensor.transpose(pb_ps[:, c, :], pb_t[:, c : c + 1].to_broadcast([P, P]), ident[:])
+
+        def gather_and_multiply(name, words, scales, row, tag):
+            picked = sb.tile([P, J], U32, name=name + "_picked", tag=tag, align_bytes=64)
+            sums = []
+            for h in range(2):
+                cols = slice(h * HALF, (h + 1) * HALF)
+                nc.vector.tensor_copy(
+                    picked[:, cols], words[:].indirect(offs_t[:, h * LIST_HALF : (h + 1) * LIST_HALF])
+                )
+                acc = ps.tile([P, HALF], F32, name=f"{name}_acc{h}")
+                nc.tensor.matmul_mx(
+                    out=acc[:],
+                    lhsT=w1_codes[:].bitcast(FP8X4),
+                    lhsT_scale=w1_scales[:],
+                    rhs=picked[:, cols].bitcast(FP8X4),
+                    rhs_scale=scales[row:P, cols],
+                    start=True,
+                    stop=True,
+                )
+                sums.append(acc)
+            return sums
+
+        a_ps = gather_and_multiply("tab", tab_w, tab_gs, 0, "tab_scales_then_picked")
+        dtab_gs = sb.tile([P, J], U8, name="dtab_gs", tag="tab_then_dtab_gs", align_bytes=64)
+        nc.vector.tensor_copy(dtab_gs[:], dtab_s[:].indirect(offs_t[:]))
+        h0 = sb.tile([P, J], F32, name="h0", tag="h0_then_wo", align_bytes=64)
+        h1 = sb.tile([P, J], F32, name="h1")
+        for h in range(2):
+            cols = slice(h * HALF, (h + 1) * HALF)
+            nc.scalar.activation(out=h0[:, cols], in_=a_ps[h][:], func=ACT.Tanh)
+            nc.scalar.activation(out=h1[:, cols], in_=h0[:, cols], func=ACT.Copy, scale=gain_t[:])
+        h0_sq = sb.tile([P, J], F32, name="h0_sq", tag="h0_sq_then_dy", align_bytes=64)
+        slope = sb.tile([P, J], F32, name="slope")
+        nc.scalar.activation(out=h0_sq[:], in_=h0[:], func=ACT.Square)
+        nc.scalar.activation(out=slope[:], in_=h0_sq[:], func=ACT.Identity, scale=neg_gain[:], bias=gain_t[:])
+
+        ta_ps = gather_and_multiply("dtab", dtab_w, dtab_gs, DTAB_ROW, "dtab_scales_then_picked")
+        base_t = sb.tile([P, J], F32, name="base_t", tag="dtab_then_base", align_bytes=64)
+        nc.sync.dma_start(out=base_t[:], in_=base)
+
+        hp = sb.tile([P, M], F32, name="hp")
+        nc.vector.tensor_copy(hp[:], h1[:].indirect(offs2_t[:]))
+        wo_inter = interleave("wo_inter", wo_raw, R, "h0_then_wo")
+
+        xh1 = sb.tile([P, J], F32, name="xh1")
+        s = sb.tile([P, M], F32, name="s")
+        nc.vector.tensor_tensor(xh1[:, 0:HALF], ta_ps[0][:], slope[:, 0:HALF], ALU.mult)
+        nc.vector.tensor_tensor(
+            s[:].rearrange("p (n c) -> p n c", c=2),
+            hp[:].rearrange("p (n c) -> p n c", c=2),
+            pb_ps[:].rearrange("p c n -> p n c"),
+            ALU.add,
+        )
+        nc.vector.tensor_tensor(xh1[:, HALF:J], ta_ps[1][:], slope[:, HALF:J], ALU.mult)
+        s_sum = group_sum("s_sum", s)
+        xs = sb.tile([P, M], F32, name="xs")
+        nc.vector.tensor_copy(xs[:], xh1[:].indirect(offs2_t[:]))
+        u = centre("u", s, s_sum, neg_k)
+        dy_inter = interleave("dy_inter", dy_raw, M, "h0_sq_then_dy")
+        th = sb.tile([P, M], F32, name="th")
+        nc.scalar.activation(out=th[:], in_=u[:], func=ACT.Tanh, scale=0.5)
+        h0p_sq = sb.tile([P, M], F32, name="h0p_sq")
+        nc.scalar.activation(out=h0p_sq[:], in_=hp[:], func=ACT.Square, scale=inv_gain[:])
+
+        xs_sum = group_sum("xs_sum", xs)
+        wo_codes, wo_scales = quantise("wo", wo_inter, R)
+        dy_codes, dy_scales = quantise("dy", dy_inter, M)
+        c0 = ps.tile([P, M], F32, name="c0")
+        nc.tensor.matmul_mx(
+            out=c0[:],
+            lhsT=wo_codes[:].bitcast(FP8X4),
+            lhsT_scale=wo_scales[:],
+            rhs=dy_codes[:].bitcast(FP8X4),
+            rhs_scale=dy_scales[:],
+            start=True,
+            stop=True,
+        )
+        w = centre("w", xs, xs_sum, neg_k)
+        b_pick = sb.tile([P, M], F32, name="b_pick")
+        nc.vector.scalar_tensor_tensor(b_pick[:], xs[:], b_fac[:], hp[:], ALU.mult, ALU.mult)
+
+        p2 = sb.tile([P, M], F32, name="p2")
+        nc.vector.scalar_tensor_tensor(p2[:], th[:], 1.0, c0[:], ALU.add, ALU.mult)
+        wt = sb.tile([P, M], F32, name="wt")
+        nc.vector.scalar_tensor_tensor(wt[:], th[:], 1.0, w[:], ALU.subtract, ALU.mult)
+        p2_sum = group_sum("p2_sum", p2)
+        q = sb.tile([P, M], F32, name="q")
+        nc.vector.scalar_tensor_tensor(q[:], wt[:], q_fac[:], p2[:], ALU.mult, ALU.mult)
+        ds2 = centre("ds2", p2, p2_sum, neg_k)
+        q_sum = group_sum("q_sum", q)
+        v1 = sb.tile([P, M], F32, name="v1")
+        nc.vector.tensor_tensor(v1[:], ds2[:], b_pick[:], ALU.mult)
+        xds = centre("xds", q, q_sum, neg_k)
+        v2 = sb.tile([P, M], F32, name="v2")
+        nc.vector.scalar_tensor_tensor(v2[:], h0p_sq[:], 1.0, xds[:], ALU.subtract, ALU.mult)
+        nc.vector.tensor_tensor(placed[:].indirect(offs2_t[:]), v1[:], v2[:], ALU.add)
+
+        y = sb.tile([P, J], F32, name="y")
+        for h, queue in enumerate((nc.sync, nc.scalar)):
+            cols = slice(h * HALF, (h + 1) * HALF)
+            nc.vector.tensor_tensor(y[:, cols], placed[:, cols], base_t[:, cols], ALU.add)
+            queue.dma_start(out=out[:, cols], in_=y[:, cols])

@@ -57,10 +57,10 @@ def tile_attend_hvcpickcentred_kernel(
         offs_t = sb.tile([P, J // 16], U16, name="offs_t")
         offs2_t = sb.tile([P, M // 16], U16, name="offs2_t")
         tab_w = sb.tile([P, T], U32, name="tab_w", tag="tab_then_dtab_gs", align_bytes=64)
-        dtab_w = sb.tile([P, T], U32, name="dtab_w", tag="dtab_then_base", align_bytes=64)
+        dtab_w = sb.tile([P, T], U32, name="dtab_w", align_bytes=64)
         tab_s = sb.tile([P, T], U8, name="tab_s", tag="tab_scales_then_picked", align_bytes=64)
         dtab_s = sb.tile([P, T], U8, name="dtab_s", tag="dtab_scales_then_picked", align_bytes=64)
-        w1_raw = sb.tile([P, PACK, R], F32, name="w1_raw", tag="weights_raw")
+        w1_raw = sb.tile([P, PACK, R], F32, name="w1_raw")
         gain_t = sb.tile([P, 1], F32, name="gain_t")
         share_t = sb.tile([P, 1], F32, name="share_t")
         og_t = sb.tile([P, 1], F32, name="og_t")
@@ -68,41 +68,50 @@ def tile_attend_hvcpickcentred_kernel(
         placed = sb.tile([P, J], F32, name="placed")
         ident = sb.tile([P, P], F32, name="ident")
 
-        nc.vector.memset(dtab_s[:].bitcast(I32), 0)
+        wo_raw = sb.tile([P, PACK, R], F32, name="wo_raw")
+        dy_raw = sb.tile([P, PACK, M], F32, name="dy_raw")
+        base_t = sb.tile([P, J], F32, name="base_t")
+
         nc.vector.memset(tab_s[:].bitcast(I32), 0)
+        nc.vector.memset(dtab_s[:].bitcast(I32), 0)
         nc.vector.memset(placed[:], 0.0)
+        make_identity(nc, ident[:])
 
         nc.sync.dma_start(offs_t[:], offs)
-        nc.scalar.dma_start(out=gain_t[:], in_=gain)
-        nc.sync.dma_start(offs2_t[:], offs2)
-        nc.scalar.dma_start(out=pb_t[:], in_=pb.rearrange("o (p c) -> (o p) c", c=2))
         nc.sync.dma_start(out=w1_raw[:], in_=w1.rearrange("(p j) r -> p j r", j=PACK))
-        nc.scalar.dma_start(out=share_t[:], in_=share)
+        nc.sync.dma_start(offs2_t[:], offs2)
+        nc.sync.dma_start(out=gain_t[:], in_=gain)
+        nc.sync.dma_start(out=pb_t[:], in_=pb.rearrange("o (p c) -> (o p) c", c=2))
         nc.sync.dma_start(out=tab_w[:].bitcast(I32), in_=tab_words[0].rearrange("p n t -> p (n t)").bitcast(I32))
-        nc.scalar.dma_start(out=og_t[:], in_=og)
-        nc.sync.dma_start(out=dtab_w[:].bitcast(I32), in_=dtab_words[0].rearrange("p n t -> p (n t)").bitcast(I32))
         for i in range(4):
             nc.scalar.dma_start(out=tab_s[i:P:32, :].bitcast(I32), in_=tab_scales[0, i:16:4, :].bitcast(I32))
-        make_identity(nc, ident[:])
+        nc.sync.dma_start(out=dtab_w[:].bitcast(I32), in_=dtab_words[0].rearrange("p n t -> p (n t)").bitcast(I32))
         for i in range(4):
-            nc.gpsimd.dma_start(
+            nc.scalar.dma_start(
                 out=dtab_s[DTAB_ROW + i : P : 32, :].bitcast(I32), in_=dtab_scales[0, i:16:4, :].bitcast(I32)
             )
+        nc.sync.dma_start(out=dy_raw[:], in_=dy.rearrange("(p j) m -> p j m", j=PACK))
+        nc.sync.dma_start(out=wo_raw[:], in_=wo.rearrange("(p j) r -> p j r", j=PACK))
+        nc.sync.dma_start(out=share_t[:], in_=share)
+        nc.sync.dma_start(out=og_t[:], in_=og)
+        nc.sync.dma_start(out=base_t[:], in_=base)
 
         neg_gain = sb.tile([P, 1], F32, name="neg_gain")
         neg_k = sb.tile([P, 1], F32, name="neg_k")
         is_tiny = sb.tile([P, 1], F32, name="is_tiny")
         safe_gain = sb.tile([P, 1], F32, name="safe_gain")
         inv_gain = sb.tile([P, 1], F32, name="inv_gain")
+        minus_one = sb.tile([P, 1], F32, name="minus_one")
+        nc.gpsimd.memset(minus_one[:], -1.0)
         q_fac = sb.tile([P, 1], F32, name="q_fac")
         b_fac = sb.tile([P, 1], F32, name="b_fac")
-        nc.vector.tensor_scalar(neg_gain[:], gain_t[:], -1.0, 0.0, ALU.mult, ALU.add)
-        nc.vector.tensor_scalar(is_tiny[:], gain_t[:], gain_t[:], TINY, ALU.mult, ALU.is_lt)
-        nc.vector.tensor_scalar(safe_gain[:], gain_t[:], is_tiny[:], 1.0, ALU.add, ALU.mult)
-        nc.vector.reciprocal(inv_gain[:], safe_gain[:])
-        nc.vector.tensor_scalar(neg_k[:], share_t[:], -1.0 / GROUP, 0.0, ALU.mult, ALU.add)
-        nc.vector.tensor_scalar(q_fac[:], og_t[:], gain_t[:], 0.25, ALU.mult, ALU.mult)
-        nc.vector.tensor_scalar(b_fac[:], og_t[:], inv_gain[:], -1.0, ALU.mult, ALU.mult)
+        nc.gpsimd.tensor_scalar(is_tiny[:], gain_t[:], gain_t[:], TINY, ALU.mult, ALU.is_lt)
+        nc.gpsimd.tensor_scalar(neg_gain[:], gain_t[:], -1.0, 0.0, ALU.mult, ALU.add)
+        nc.gpsimd.tensor_scalar(safe_gain[:], gain_t[:], is_tiny[:], 1.0, ALU.add, ALU.mult)
+        nc.gpsimd.tensor_scalar(neg_k[:], share_t[:], -1.0 / GROUP, 0.0, ALU.mult, ALU.add)
+        nc.gpsimd.tensor_scalar(q_fac[:], og_t[:], gain_t[:], 0.25, ALU.mult, ALU.mult)
+        nc.gpsimd.tensor_tensor(inv_gain[:], safe_gain[:], minus_one[:], ALU.pow)
+        nc.gpsimd.tensor_scalar(b_fac[:], og_t[:], inv_gain[:], -1.0, ALU.mult, ALU.mult)
 
         def interleave(name, raw, width, tag):
             inter = sb.tile([P, width, PACK], BF16, name=name, tag=tag, align_bytes=64)
@@ -117,14 +126,11 @@ def tile_attend_hvcpickcentred_kernel(
             )
             return codes, scales
 
-        w1_inter = interleave("w1_inter", w1_raw, R, "w1_inter_then_dy")
-        wo_raw = sb.tile([P, PACK, R], F32, name="wo_raw", tag="weights_raw")
-        nc.sync.dma_start(out=wo_raw[:], in_=wo.rearrange("(p j) r -> p j r", j=PACK))
+        w1_inter = sb.tile([P, R, PACK], BF16, name="w1_inter", align_bytes=64)
+        nc.vector.tensor_copy(out=w1_inter[:], in_=w1_raw[:].rearrange("p j w -> p w j"))
         tab_gs = sb.tile([P, J], U8, name="tab_gs", align_bytes=64)
         nc.vector.tensor_copy(tab_gs[:], tab_s[:].indirect(offs_t[:]))
         w1_codes, w1_scales = quantise("w1", w1_inter, R)
-        dy_raw = sb.tile([P, PACK, M], F32, name="dy_raw", tag="w1_inter_then_dy", align_bytes=64)
-        nc.sync.dma_start(out=dy_raw[:], in_=dy.rearrange("(p j) m -> p j m", j=PACK))
 
         pb_ps = ps.tile([P, 2, P], F32, name="pb_ps")
         for c in range(2):
@@ -166,12 +172,11 @@ def tile_attend_hvcpickcentred_kernel(
         nc.scalar.activation(out=slope[:], in_=h0_sq[:], func=ACT.Identity, scale=neg_gain[:], bias=gain_t[:])
 
         ta_ps = gather_and_multiply("dtab", dtab_w, dtab_gs, DTAB_ROW, "dtab_scales_then_picked")
-        base_t = sb.tile([P, J], F32, name="base_t", tag="dtab_then_base", align_bytes=64)
-        nc.sync.dma_start(out=base_t[:], in_=base)
 
         hp = sb.tile([P, M], F32, name="hp")
         nc.vector.tensor_copy(hp[:], h1[:].indirect(offs2_t[:]))
-        wo_inter = interleave("wo_inter", wo_raw, R, "h0_then_wo")
+        dy_inter = interleave("dy_inter", dy_raw, M, "h0_then_wo")
+        wo_inter = interleave("wo_inter", wo_raw, R, "h0_sq_then_dy")
 
         xh1 = sb.tile([P, J], F32, name="xh1")
         s = sb.tile([P, M], F32, name="s")
@@ -184,18 +189,14 @@ def tile_attend_hvcpickcentred_kernel(
         )
         nc.vector.tensor_tensor(xh1[:, HALF:J], ta_ps[1][:], slope[:, HALF:J], ALU.mult)
         s_sum = group_sum("s_sum", s)
-        xs = sb.tile([P, M], F32, name="xs")
-        nc.vector.tensor_copy(xs[:], xh1[:].indirect(offs2_t[:]))
         u = centre("u", s, s_sum, neg_k)
-        dy_inter = interleave("dy_inter", dy_raw, M, "h0_sq_then_dy")
         th = sb.tile([P, M], F32, name="th")
         nc.scalar.activation(out=th[:], in_=u[:], func=ACT.Tanh, scale=0.5)
         h0p_sq = sb.tile([P, M], F32, name="h0p_sq")
         nc.scalar.activation(out=h0p_sq[:], in_=hp[:], func=ACT.Square, scale=inv_gain[:])
 
-        xs_sum = group_sum("xs_sum", xs)
-        wo_codes, wo_scales = quantise("wo", wo_inter, R)
         dy_codes, dy_scales = quantise("dy", dy_inter, M)
+        wo_codes, wo_scales = quantise("wo", wo_inter, R)
         c0 = ps.tile([P, M], F32, name="c0")
         nc.tensor.matmul_mx(
             out=c0[:],
@@ -206,22 +207,25 @@ def tile_attend_hvcpickcentred_kernel(
             start=True,
             stop=True,
         )
-        w = centre("w", xs, xs_sum, neg_k)
-        b_pick = sb.tile([P, M], F32, name="b_pick")
-        nc.vector.scalar_tensor_tensor(b_pick[:], xs[:], b_fac[:], hp[:], ALU.mult, ALU.mult)
+        xs = sb.tile([P, M], F32, name="xs", tag="h0_sq_then_dy", align_bytes=64)
+        nc.vector.tensor_copy(xs[:], xh1[:].indirect(offs2_t[:]))
 
+        xs_sum = group_sum("xs_sum", xs)
         p2 = sb.tile([P, M], F32, name="p2")
         nc.vector.scalar_tensor_tensor(p2[:], th[:], 1.0, c0[:], ALU.add, ALU.mult)
-        wt = sb.tile([P, M], F32, name="wt")
-        nc.vector.scalar_tensor_tensor(wt[:], th[:], 1.0, w[:], ALU.subtract, ALU.mult)
+        w = centre("w", xs, xs_sum, neg_k)
+        curve = sb.tile([P, M], F32, name="curve")
+        nc.vector.scalar_tensor_tensor(curve[:], th[:], 1.0, p2[:], ALU.subtract, ALU.mult)
         p2_sum = group_sum("p2_sum", p2)
         q = sb.tile([P, M], F32, name="q")
-        nc.vector.scalar_tensor_tensor(q[:], wt[:], q_fac[:], p2[:], ALU.mult, ALU.mult)
+        nc.vector.scalar_tensor_tensor(q[:], w[:], q_fac[:], curve[:], ALU.mult, ALU.mult)
         ds2 = centre("ds2", p2, p2_sum, neg_k)
         q_sum = group_sum("q_sum", q)
-        v1 = sb.tile([P, M], F32, name="v1")
-        nc.vector.tensor_tensor(v1[:], ds2[:], b_pick[:], ALU.mult)
+        hd = sb.tile([P, M], F32, name="hd")
+        nc.vector.scalar_tensor_tensor(hd[:], ds2[:], b_fac[:], hp[:], ALU.mult, ALU.mult)
         xds = centre("xds", q, q_sum, neg_k)
+        v1 = sb.tile([P, M], F32, name="v1")
+        nc.vector.tensor_tensor(v1[:], hd[:], xs[:], ALU.mult)
         v2 = sb.tile([P, M], F32, name="v2")
         nc.vector.scalar_tensor_tensor(v2[:], h0p_sq[:], 1.0, xds[:], ALU.subtract, ALU.mult)
         nc.vector.tensor_tensor(placed[:].indirect(offs2_t[:]), v1[:], v2[:], ALU.add)

@@ -1,7 +1,6 @@
 from contextlib import ExitStack
 
 import concourse.mybir as mybir
-from concourse.masks import make_identity
 
 K, R, F, T, J, M, G = 512, 128, 512, 2048, 512, 256, 32
 FLOPS = 2 * K * R * J * 2 + 2 * F * R * M
@@ -19,6 +18,7 @@ AX = mybir.AxisListType
 
 P = 128
 PACK = 4
+QUAD = 32
 GROUP = M // G
 HALF = J // 2
 LIST_HALF = HALF // 16
@@ -32,6 +32,7 @@ def tile_attend_hvcpickcentred_kernel(
     nc = tc.nc
     with ExitStack() as ctx:
         sb = ctx.enter_context(tc.tile_pool(name="sb", bufs=1))
+        shared = ctx.enter_context(tc.tile_pool(name="shared", bufs=1))
         ps = ctx.enter_context(tc.psum_pool(name="ps", bufs=1))
 
         def grouped(t):
@@ -56,45 +57,61 @@ def tile_attend_hvcpickcentred_kernel(
 
         offs_t = sb.tile([P, J // 16], U16, name="offs_t")
         offs2_t = sb.tile([P, M // 16], U16, name="offs2_t")
-        tab_w = sb.tile([P, T], U32, name="tab_w", tag="tab_then_dtab_gs", align_bytes=64)
-        dtab_w = sb.tile([P, T], U32, name="dtab_w", align_bytes=64)
         tab_s = sb.tile([P, T], U8, name="tab_s", tag="tab_scales_then_picked", align_bytes=64)
         dtab_s = sb.tile([P, T], U8, name="dtab_s", tag="dtab_scales_then_picked", align_bytes=64)
-        w1_raw = sb.tile([P, PACK, R], F32, name="w1_raw")
-        gain_t = sb.tile([P, 1], F32, name="gain_t")
-        share_t = sb.tile([P, 1], F32, name="share_t")
-        og_t = sb.tile([P, 1], F32, name="og_t")
-        pb_t = sb.tile([P, 2], F32, name="pb_t")
+        w1_raw = shared.tile([P, PACK, R], F32, name="w1_raw", offset=7168, align_bytes=64)
         placed = sb.tile([P, J], F32, name="placed")
         ident = sb.tile([P, P], F32, name="ident")
 
-        wo_raw = sb.tile([P, PACK, R], F32, name="wo_raw")
-        dy_raw = sb.tile([P, PACK, M], F32, name="dy_raw")
-        base_t = sb.tile([P, J], F32, name="base_t")
-
+        ones = sb.tile([P, QUAD], F32, name="ones", tag="tab_then_dtab_gs", align_bytes=64)
+        col_count = sb.tile([P, QUAD], F32, name="col_count", align_bytes=64)
+        row_count = sb.tile([P, QUAD], F32, name="row_count", align_bytes=64)
+        nc.vector.memset(ones[:], 1.0)
         nc.vector.memset(tab_s[:].bitcast(I32), 0)
+        nc.vector.tensor_tensor_scan(col_count[:], ones[:], ones[:], 0.0, ALU.mult, ALU.add)
         nc.vector.memset(dtab_s[:].bitcast(I32), 0)
-        nc.vector.memset(placed[:], 0.0)
-        make_identity(nc, ident[:])
+        nc.vector.transpose(row_count[:], col_count[:])
+        nc.gpsimd.memset(ident[:], 0.0)
+        for q0 in range(0, P, QUAD):
+            rows = slice(q0, q0 + QUAD)
+            nc.vector.tensor_tensor(ident[rows, rows], col_count[rows, :], row_count[rows, :], ALU.is_equal)
+        nc.gpsimd.memset(placed[:], 0.0)
 
-        nc.sync.dma_start(offs_t[:], offs)
         nc.sync.dma_start(out=w1_raw[:], in_=w1.rearrange("(p j) r -> p j r", j=PACK))
+        nc.sync.dma_start(offs_t[:], offs)
         nc.sync.dma_start(offs2_t[:], offs2)
-        nc.sync.dma_start(out=gain_t[:], in_=gain)
-        nc.sync.dma_start(out=pb_t[:], in_=pb.rearrange("o (p c) -> (o p) c", c=2))
+        for i, queue in enumerate((nc.sync, nc.scalar, nc.sync, nc.scalar)):
+            queue.dma_start(out=tab_s[i:P:32, :].bitcast(I32), in_=tab_scales[0, i:16:4, :].bitcast(I32))
+        tab_w = sb.tile([P, T], U32, name="tab_w", tag="tab_then_dtab_gs", align_bytes=64)
         nc.sync.dma_start(out=tab_w[:].bitcast(I32), in_=tab_words[0].rearrange("p n t -> p (n t)").bitcast(I32))
         for i in range(4):
-            nc.scalar.dma_start(out=tab_s[i:P:32, :].bitcast(I32), in_=tab_scales[0, i:16:4, :].bitcast(I32))
-        nc.sync.dma_start(out=dtab_w[:].bitcast(I32), in_=dtab_words[0].rearrange("p n t -> p (n t)").bitcast(I32))
-        for i in range(4):
-            nc.scalar.dma_start(
+            nc.sync.dma_start(
                 out=dtab_s[DTAB_ROW + i : P : 32, :].bitcast(I32), in_=dtab_scales[0, i:16:4, :].bitcast(I32)
             )
-        nc.sync.dma_start(out=dy_raw[:], in_=dy.rearrange("(p j) m -> p j m", j=PACK))
-        nc.sync.dma_start(out=wo_raw[:], in_=wo.rearrange("(p j) r -> p j r", j=PACK))
-        nc.sync.dma_start(out=share_t[:], in_=share)
-        nc.sync.dma_start(out=og_t[:], in_=og)
-        nc.sync.dma_start(out=base_t[:], in_=base)
+
+        def interleave(inter, raw):
+            nc.scalar.activation(out=inter[:], in_=raw[:].rearrange("p j w -> p w j"), func=ACT.Copy)
+
+        def quantise(name, inter, width):
+            codes = sb.tile([P, width], U32, name=name + "_codes", align_bytes=64)
+            scales = sb.tile([P, width], U8, name=name + "_scales", align_bytes=64)
+            nc.vector.quantize_mx(
+                out=codes[:].bitcast(FP8X4), scales=scales[:], in_=inter[:].rearrange("p w j -> p (w j)")
+            )
+            return codes, scales
+
+        w1_inter = shared.tile([P, R, PACK], BF16, name="w1_inter", offset=10368 + 4096 - 512, align_bytes=64)
+        nc.vector.tensor_copy(out=w1_inter[:], in_=w1_raw[:].rearrange("p j w -> p w j"))
+
+        dtab_w = shared.tile([P, T], U32, name="dtab_w", offset=0, align_bytes=64)
+        vectors = shared.tile([P, 4, 8], F32, name="vectors", offset=8192, align_bytes=64)
+        gain_t, share_t, og_t = vectors[:, 0, 0:1], vectors[:, 1, 0:1], vectors[:, 2, 0:1]
+        pb_t = vectors[:, 3, 0:2]
+        nc.sync.dma_start(out=gain_t, in_=gain)
+        nc.sync.dma_start(out=pb_t, in_=pb.rearrange("o (p c) -> (o p) c", c=2))
+        nc.sync.dma_start(out=dtab_w[:].bitcast(I32), in_=dtab_words[0].rearrange("p n t -> p (n t)").bitcast(I32))
+        nc.sync.dma_start(out=share_t, in_=share)
+        nc.sync.dma_start(out=og_t, in_=og)
 
         neg_gain = sb.tile([P, 1], F32, name="neg_gain")
         neg_k = sb.tile([P, 1], F32, name="neg_k")
@@ -105,32 +122,21 @@ def tile_attend_hvcpickcentred_kernel(
         nc.gpsimd.memset(minus_one[:], -1.0)
         q_fac = sb.tile([P, 1], F32, name="q_fac")
         b_fac = sb.tile([P, 1], F32, name="b_fac")
-        nc.gpsimd.tensor_scalar(is_tiny[:], gain_t[:], gain_t[:], TINY, ALU.mult, ALU.is_lt)
-        nc.gpsimd.tensor_scalar(neg_gain[:], gain_t[:], -1.0, 0.0, ALU.mult, ALU.add)
-        nc.gpsimd.tensor_scalar(safe_gain[:], gain_t[:], is_tiny[:], 1.0, ALU.add, ALU.mult)
-        nc.gpsimd.tensor_scalar(neg_k[:], share_t[:], -1.0 / GROUP, 0.0, ALU.mult, ALU.add)
-        nc.gpsimd.tensor_scalar(q_fac[:], og_t[:], gain_t[:], 0.25, ALU.mult, ALU.mult)
+        nc.gpsimd.tensor_scalar(is_tiny[:], gain_t, gain_t, TINY, ALU.mult, ALU.is_lt)
+        nc.gpsimd.tensor_scalar(neg_gain[:], gain_t, -1.0, 0.0, ALU.mult, ALU.add)
+        nc.gpsimd.tensor_scalar(safe_gain[:], gain_t, is_tiny[:], 1.0, ALU.add, ALU.mult)
+        nc.gpsimd.tensor_scalar(neg_k[:], share_t, -1.0 / GROUP, 0.0, ALU.mult, ALU.add)
+        nc.gpsimd.tensor_scalar(q_fac[:], og_t, gain_t, 0.25, ALU.mult, ALU.mult)
         nc.gpsimd.tensor_tensor(inv_gain[:], safe_gain[:], minus_one[:], ALU.pow)
-        nc.gpsimd.tensor_scalar(b_fac[:], og_t[:], inv_gain[:], -1.0, ALU.mult, ALU.mult)
+        nc.gpsimd.tensor_scalar(b_fac[:], og_t, inv_gain[:], -1.0, ALU.mult, ALU.mult)
 
-        def interleave(name, raw, width, tag):
-            inter = sb.tile([P, width, PACK], BF16, name=name, tag=tag, align_bytes=64)
-            nc.scalar.activation(out=inter[:], in_=raw[:].rearrange("p j w -> p w j"), func=ACT.Copy)
-            return inter
-
-        def quantise(name, inter, width):
-            codes = sb.tile([P, width], U32, name=name + "_codes", align_bytes=64)
-            scales = sb.tile([P, width], U8, name=name + "_scales", align_bytes=64)
-            nc.vector.quantize_mx(
-                out=codes[:].bitcast(FP8X4), scales=scales[:], in_=inter[:].rearrange("p w j -> p (w j)")
-            )
-            return codes, scales
-
-        w1_inter = sb.tile([P, R, PACK], BF16, name="w1_inter", align_bytes=64)
-        nc.vector.tensor_copy(out=w1_inter[:], in_=w1_raw[:].rearrange("p j w -> p w j"))
-        tab_gs = sb.tile([P, J], U8, name="tab_gs", align_bytes=64)
+        tab_gs = sb.tile([P, J], U8, name="tab_gs", tag="tab_gs_then_base", align_bytes=64)
         nc.vector.tensor_copy(tab_gs[:], tab_s[:].indirect(offs_t[:]))
         w1_codes, w1_scales = quantise("w1", w1_inter, R)
+        dy_raw = shared.tile([P, PACK, M], F32, name="dy_raw", offset=10368, align_bytes=64)
+        wo_raw = shared.tile([P, PACK, R], F32, name="wo_raw", offset=10368 + 4096, align_bytes=64)
+        nc.sync.dma_start(out=dy_raw[:], in_=dy.rearrange("(p j) m -> p j m", j=PACK))
+        nc.sync.dma_start(out=wo_raw[:], in_=wo.rearrange("(p j) r -> p j r", j=PACK))
 
         pb_ps = ps.tile([P, 2, P], F32, name="pb_ps")
         for c in range(2):
@@ -158,25 +164,30 @@ def tile_attend_hvcpickcentred_kernel(
             return sums
 
         a_ps = gather_and_multiply("tab", tab_w, tab_gs, 0, "tab_scales_then_picked")
+        base_t = sb.tile([P, J], F32, name="base_t", tag="tab_gs_then_base", align_bytes=64)
+        nc.sync.dma_start(out=base_t[:], in_=base)
         dtab_gs = sb.tile([P, J], U8, name="dtab_gs", tag="tab_then_dtab_gs", align_bytes=64)
         nc.vector.tensor_copy(dtab_gs[:], dtab_s[:].indirect(offs_t[:]))
-        h0 = sb.tile([P, J], F32, name="h0", tag="h0_then_wo", align_bytes=64)
+        h0 = sb.tile([P, J], F32, name="h0", tag="h0_then_dy", align_bytes=64)
         h1 = sb.tile([P, J], F32, name="h1")
         for h in range(2):
             cols = slice(h * HALF, (h + 1) * HALF)
             nc.scalar.activation(out=h0[:, cols], in_=a_ps[h][:], func=ACT.Tanh)
-            nc.scalar.activation(out=h1[:, cols], in_=h0[:, cols], func=ACT.Copy, scale=gain_t[:])
-        h0_sq = sb.tile([P, J], F32, name="h0_sq", tag="h0_sq_then_dy", align_bytes=64)
+            nc.scalar.activation(out=h1[:, cols], in_=h0[:, cols], func=ACT.Copy, scale=gain_t)
+        h0_sq = sb.tile([P, J], F32, name="h0_sq", tag="h0_sq_wo_xs", align_bytes=64)
         slope = sb.tile([P, J], F32, name="slope")
         nc.scalar.activation(out=h0_sq[:], in_=h0[:], func=ACT.Square)
-        nc.scalar.activation(out=slope[:], in_=h0_sq[:], func=ACT.Identity, scale=neg_gain[:], bias=gain_t[:])
+        nc.scalar.activation(out=slope[:], in_=h0_sq[:], func=ACT.Identity, scale=neg_gain[:], bias=gain_t)
+
+        dy_inter = sb.tile([P, M, PACK], BF16, name="dy_inter", tag="h0_then_dy", align_bytes=64)
+        wo_inter = sb.tile([P, R, PACK], BF16, name="wo_inter", tag="h0_sq_wo_xs", align_bytes=64)
+        interleave(dy_inter, dy_raw)
+        interleave(wo_inter, wo_raw)
 
         ta_ps = gather_and_multiply("dtab", dtab_w, dtab_gs, DTAB_ROW, "dtab_scales_then_picked")
 
-        hp = sb.tile([P, M], F32, name="hp")
+        hp = shared.tile([P, M], F32, name="hp", offset=0, align_bytes=64)
         nc.vector.tensor_copy(hp[:], h1[:].indirect(offs2_t[:]))
-        dy_inter = interleave("dy_inter", dy_raw, M, "h0_then_wo")
-        wo_inter = interleave("wo_inter", wo_raw, R, "h0_sq_then_dy")
 
         xh1 = sb.tile([P, J], F32, name="xh1")
         s = sb.tile([P, M], F32, name="s")
@@ -190,9 +201,9 @@ def tile_attend_hvcpickcentred_kernel(
         nc.vector.tensor_tensor(xh1[:, HALF:J], ta_ps[1][:], slope[:, HALF:J], ALU.mult)
         s_sum = group_sum("s_sum", s)
         u = centre("u", s, s_sum, neg_k)
-        th = sb.tile([P, M], F32, name="th")
+        th = shared.tile([P, M], F32, name="th", offset=10368 + 4096, align_bytes=64)
         nc.scalar.activation(out=th[:], in_=u[:], func=ACT.Tanh, scale=0.5)
-        h0p_sq = sb.tile([P, M], F32, name="h0p_sq")
+        h0p_sq = shared.tile([P, M], F32, name="h0p_sq", offset=10368 + 4096 + 1024, align_bytes=64)
         nc.scalar.activation(out=h0p_sq[:], in_=hp[:], func=ACT.Square, scale=inv_gain[:])
 
         dy_codes, dy_scales = quantise("dy", dy_inter, M)
@@ -207,7 +218,7 @@ def tile_attend_hvcpickcentred_kernel(
             start=True,
             stop=True,
         )
-        xs = sb.tile([P, M], F32, name="xs", tag="h0_sq_then_dy", align_bytes=64)
+        xs = sb.tile([P, M], F32, name="xs", tag="h0_sq_wo_xs", align_bytes=64)
         nc.vector.tensor_copy(xs[:], xh1[:].indirect(offs2_t[:]))
 
         xs_sum = group_sum("xs_sum", xs)

@@ -33,27 +33,24 @@ def tile_attend_hvcpickcentred_kernel(
     with ExitStack() as ctx:
         sb = ctx.enter_context(tc.tile_pool(name="sb", bufs=1))
         shared = ctx.enter_context(tc.tile_pool(name="shared", bufs=1))
+        mid = ctx.enter_context(tc.tile_pool(name="mid", bufs=1))
         ps = ctx.enter_context(tc.psum_pool(name="ps", bufs=1))
 
         def grouped(t):
             return t.rearrange("p (g e) -> p g e", e=GROUP)
 
-        def group_sum(name, x):
-            total = sb.tile([P, G], F32, name=name)
-            nc.vector.tensor_reduce(out=total[:], in_=grouped(x[:]), axis=AX.X, op=ALU.add)
-            return total
+        def group_sum(total, x):
+            nc.vector.tensor_reduce(out=total, in_=grouped(x), axis=AX.X, op=ALU.add)
 
-        def centre(name, x, total, neg_k):
-            res = sb.tile([P, M], F32, name=name)
+        def centre(res, x, total, neg_k):
             nc.vector.scalar_tensor_tensor(
-                out=grouped(res[:]),
-                in0=total[:].unsqueeze(2).to_broadcast([P, G, GROUP]),
+                out=grouped(res),
+                in0=total.unsqueeze(2).to_broadcast([P, total.shape[1], GROUP]),
                 scalar=neg_k[:],
-                in1=grouped(x[:]),
+                in1=grouped(x),
                 op0=ALU.mult,
                 op1=ALU.add,
             )
-            return res
 
         offs_t = sb.tile([P, J // 16], U16, name="offs_t")
         offs2_t = sb.tile([P, M // 16], U16, name="offs2_t")
@@ -71,11 +68,11 @@ def tile_attend_hvcpickcentred_kernel(
         nc.vector.tensor_tensor_scan(col_count[:], ones[:], ones[:], 0.0, ALU.mult, ALU.add)
         nc.vector.memset(dtab_s[:].bitcast(I32), 0)
         nc.vector.transpose(row_count[:], col_count[:])
-        nc.gpsimd.memset(ident[:], 0.0)
+        nc.vector.memset(ident[:], 0.0)
         for q0 in range(0, P, QUAD):
             rows = slice(q0, q0 + QUAD)
             nc.vector.tensor_tensor(ident[rows, rows], col_count[rows, :], row_count[rows, :], ALU.is_equal)
-        nc.gpsimd.memset(placed[:], 0.0)
+        nc.vector.memset(placed[:], 0.0)
 
         nc.sync.dma_start(out=w1_raw[:], in_=w1.rearrange("(p j) r -> p j r", j=PACK))
         nc.sync.dma_start(offs_t[:], offs)
@@ -114,21 +111,17 @@ def tile_attend_hvcpickcentred_kernel(
         nc.sync.dma_start(out=og_t, in_=og)
 
         neg_gain = sb.tile([P, 1], F32, name="neg_gain")
-        neg_k = sb.tile([P, 1], F32, name="neg_k")
+        quarter_gain = sb.tile([P, 1], F32, name="quarter_gain")
         is_tiny = sb.tile([P, 1], F32, name="is_tiny")
         safe_gain = sb.tile([P, 1], F32, name="safe_gain")
         inv_gain = sb.tile([P, 1], F32, name="inv_gain")
         minus_one = sb.tile([P, 1], F32, name="minus_one")
-        nc.gpsimd.memset(minus_one[:], -1.0)
-        q_fac = sb.tile([P, 1], F32, name="q_fac")
-        b_fac = sb.tile([P, 1], F32, name="b_fac")
+        nc.scalar.activation(out=neg_gain[:], in_=gain_t, func=ACT.Copy, scale=-1.0)
+        nc.scalar.activation(out=quarter_gain[:], in_=gain_t, func=ACT.Copy, scale=0.25)
+        nc.vector.memset(minus_one[:], -1.0)
         nc.gpsimd.tensor_scalar(is_tiny[:], gain_t, gain_t, TINY, ALU.mult, ALU.is_lt)
-        nc.gpsimd.tensor_scalar(neg_gain[:], gain_t, -1.0, 0.0, ALU.mult, ALU.add)
         nc.gpsimd.tensor_scalar(safe_gain[:], gain_t, is_tiny[:], 1.0, ALU.add, ALU.mult)
-        nc.gpsimd.tensor_scalar(neg_k[:], share_t, -1.0 / GROUP, 0.0, ALU.mult, ALU.add)
-        nc.gpsimd.tensor_scalar(q_fac[:], og_t, gain_t, 0.25, ALU.mult, ALU.mult)
         nc.gpsimd.tensor_tensor(inv_gain[:], safe_gain[:], minus_one[:], ALU.pow)
-        nc.gpsimd.tensor_scalar(b_fac[:], og_t, inv_gain[:], -1.0, ALU.mult, ALU.mult)
 
         tab_gs = sb.tile([P, J], U8, name="tab_gs", tag="tab_gs_then_base", align_bytes=64)
         nc.vector.tensor_copy(tab_gs[:], tab_s[:].indirect(offs_t[:]))
@@ -138,21 +131,15 @@ def tile_attend_hvcpickcentred_kernel(
         nc.sync.dma_start(out=dy_raw[:], in_=dy.rearrange("(p j) m -> p j m", j=PACK))
         nc.sync.dma_start(out=wo_raw[:], in_=wo.rearrange("(p j) r -> p j r", j=PACK))
 
-        pb_ps = ps.tile([P, 2, P], F32, name="pb_ps")
-        for c in range(2):
-            nc.tensor.transpose(pb_ps[:, c, :], pb_t[:, c : c + 1].to_broadcast([P, P]), ident[:])
-
-        def gather_and_multiply(name, words, scales, row, tag):
+        def gather_and_multiply(name, words, scales, row, tag, sums):
             picked = sb.tile([P, J], U32, name=name + "_picked", tag=tag, align_bytes=64)
-            sums = []
             for h in range(2):
                 cols = slice(h * HALF, (h + 1) * HALF)
                 nc.vector.tensor_copy(
                     picked[:, cols], words[:].indirect(offs_t[:, h * LIST_HALF : (h + 1) * LIST_HALF])
                 )
-                acc = ps.tile([P, HALF], F32, name=f"{name}_acc{h}")
                 nc.tensor.matmul_mx(
-                    out=acc[:],
+                    out=sums[h],
                     lhsT=w1_codes[:].bitcast(FP8X4),
                     lhsT_scale=w1_scales[:],
                     rhs=picked[:, cols].bitcast(FP8X4),
@@ -160,50 +147,66 @@ def tile_attend_hvcpickcentred_kernel(
                     start=True,
                     stop=True,
                 )
-                sums.append(acc)
-            return sums
 
-        a_ps = gather_and_multiply("tab", tab_w, tab_gs, 0, "tab_scales_then_picked")
+        a_lo = ps.tile([P, HALF], F32, name="a_lo", tag="a_lo_then_pb")
+        a_hi = ps.tile([P, HALF], F32, name="a_hi")
+        a_ps = (a_lo[:], a_hi[:])
+        gather_and_multiply("tab", tab_w, tab_gs, 0, "tab_scales_then_picked", a_ps)
         base_t = sb.tile([P, J], F32, name="base_t", tag="tab_gs_then_base", align_bytes=64)
         nc.sync.dma_start(out=base_t[:], in_=base)
         dtab_gs = sb.tile([P, J], U8, name="dtab_gs", tag="tab_then_dtab_gs", align_bytes=64)
         nc.vector.tensor_copy(dtab_gs[:], dtab_s[:].indirect(offs_t[:]))
-        h0 = sb.tile([P, J], F32, name="h0", tag="h0_then_dy", align_bytes=64)
+        h0 = sb.tile([P, J], F32, name="h0")
         h1 = sb.tile([P, J], F32, name="h1")
         for h in range(2):
             cols = slice(h * HALF, (h + 1) * HALF)
-            nc.scalar.activation(out=h0[:, cols], in_=a_ps[h][:], func=ACT.Tanh)
+            nc.scalar.activation(out=h0[:, cols], in_=a_ps[h], func=ACT.Tanh)
             nc.scalar.activation(out=h1[:, cols], in_=h0[:, cols], func=ACT.Copy, scale=gain_t)
-        h0_sq = sb.tile([P, J], F32, name="h0_sq", tag="h0_sq_wo_xs", align_bytes=64)
+        pb_ta = ps.tile([P, M + HALF], F32, name="pb_ta", tag="a_lo_then_pb")
+        pb_ps = pb_ta[:, 0:M].rearrange("p (c n) -> p c n", c=2)
+        for c in range(2):
+            nc.tensor.transpose(pb_ps[:, c, :], pb_t[:, c : c + 1].to_broadcast([P, P]), ident[:])
+
+        h0_sq = mid.tile([P, J], F32, name="h0_sq", offset=1088, align_bytes=64)
         slope = sb.tile([P, J], F32, name="slope")
         nc.scalar.activation(out=h0_sq[:], in_=h0[:], func=ACT.Square)
         nc.scalar.activation(out=slope[:], in_=h0_sq[:], func=ACT.Identity, scale=neg_gain[:], bias=gain_t)
 
-        dy_inter = sb.tile([P, M, PACK], BF16, name="dy_inter", tag="h0_then_dy", align_bytes=64)
-        wo_inter = sb.tile([P, R, PACK], BF16, name="wo_inter", tag="h0_sq_wo_xs", align_bytes=64)
+        neg_k = mid.tile([P, 1], F32, name="neg_k", offset=3072, align_bytes=64)
+        nc.scalar.activation(out=neg_k[:], in_=share_t, func=ACT.Copy, scale=-1.0 / GROUP)
+        dy_inter = mid.tile([P, M, PACK], BF16, name="dy_inter", offset=0, align_bytes=64)
+        wo_inter = mid.tile([P, R, PACK], BF16, name="wo_inter", offset=2048, align_bytes=64)
         interleave(dy_inter, dy_raw)
         interleave(wo_inter, wo_raw)
 
-        ta_ps = gather_and_multiply("dtab", dtab_w, dtab_gs, DTAB_ROW, "dtab_scales_then_picked")
+        ta_hi = ps.tile([P, HALF], F32, name="ta_hi")
+        ta_ps = (pb_ta[:, M : M + HALF], ta_hi[:])
+        gather_and_multiply("dtab", dtab_w, dtab_gs, DTAB_ROW, "dtab_scales_then_picked", ta_ps)
 
         hp = shared.tile([P, M], F32, name="hp", offset=0, align_bytes=64)
         nc.vector.tensor_copy(hp[:], h1[:].indirect(offs2_t[:]))
 
         xh1 = sb.tile([P, J], F32, name="xh1")
         s = sb.tile([P, M], F32, name="s")
-        nc.vector.tensor_tensor(xh1[:, 0:HALF], ta_ps[0][:], slope[:, 0:HALF], ALU.mult)
+        nc.vector.tensor_tensor(xh1[:, 0:HALF], ta_ps[0], slope[:, 0:HALF], ALU.mult)
         nc.vector.tensor_tensor(
             s[:].rearrange("p (n c) -> p n c", c=2),
             hp[:].rearrange("p (n c) -> p n c", c=2),
-            pb_ps[:].rearrange("p c n -> p n c"),
+            pb_ps.rearrange("p c n -> p n c"),
             ALU.add,
         )
-        nc.vector.tensor_tensor(xh1[:, HALF:J], ta_ps[1][:], slope[:, HALF:J], ALU.mult)
-        s_sum = group_sum("s_sum", s)
-        u = centre("u", s, s_sum, neg_k)
-        th = shared.tile([P, M], F32, name="th", offset=10368 + 4096, align_bytes=64)
+        nc.vector.tensor_tensor(xh1[:, HALF:J], ta_ps[1], slope[:, HALF:J], ALU.mult)
+        s_sum = sb.tile([P, G], F32, name="s_sum")
+        group_sum(s_sum[:], s[:])
+        xs = sb.tile([P, M], F32, name="xs")
+        nc.vector.tensor_copy(xs[:], xh1[:].indirect(offs2_t[:]))
+        u = sb.tile([P, M], F32, name="u")
+        centre(u[:], s[:], s_sum[:], neg_k)
+        th = shared.tile([P, M], F32, name="th", offset=10368 + 4096 + 512, align_bytes=64)
         nc.scalar.activation(out=th[:], in_=u[:], func=ACT.Tanh, scale=0.5)
-        h0p_sq = shared.tile([P, M], F32, name="h0p_sq", offset=10368 + 4096 + 1024, align_bytes=64)
+        h0p_sq = shared.tile([P, M], F32, name="h0p_sq", offset=10368 + 4096 + 1536, align_bytes=64)
+        h0p = shared.tile([P, M], F32, name="h0p", offset=10368 + 4096 - 512, align_bytes=64)
+        nc.scalar.activation(out=h0p[:], in_=hp[:], func=ACT.Copy, scale=inv_gain[:])
         nc.scalar.activation(out=h0p_sq[:], in_=hp[:], func=ACT.Square, scale=inv_gain[:])
 
         dy_codes, dy_scales = quantise("dy", dy_inter, M)
@@ -218,31 +221,36 @@ def tile_attend_hvcpickcentred_kernel(
             start=True,
             stop=True,
         )
-        xs = sb.tile([P, M], F32, name="xs", tag="h0_sq_wo_xs", align_bytes=64)
-        nc.vector.tensor_copy(xs[:], xh1[:].indirect(offs2_t[:]))
 
-        xs_sum = group_sum("xs_sum", xs)
-        p2 = sb.tile([P, M], F32, name="p2")
-        nc.vector.scalar_tensor_tensor(p2[:], th[:], 1.0, c0[:], ALU.add, ALU.mult)
-        w = centre("w", xs, xs_sum, neg_k)
-        curve = sb.tile([P, M], F32, name="curve")
-        nc.vector.scalar_tensor_tensor(curve[:], th[:], 1.0, p2[:], ALU.subtract, ALU.mult)
-        p2_sum = group_sum("p2_sum", p2)
-        q = sb.tile([P, M], F32, name="q")
-        nc.vector.scalar_tensor_tensor(q[:], w[:], q_fac[:], curve[:], ALU.mult, ALU.mult)
-        ds2 = centre("ds2", p2, p2_sum, neg_k)
-        q_sum = group_sum("q_sum", q)
-        hd = sb.tile([P, M], F32, name="hd")
-        nc.vector.scalar_tensor_tensor(hd[:], ds2[:], b_fac[:], hp[:], ALU.mult, ALU.mult)
-        xds = centre("xds", q, q_sum, neg_k)
-        v1 = sb.tile([P, M], F32, name="v1")
-        nc.vector.tensor_tensor(v1[:], hd[:], xs[:], ALU.mult)
-        v2 = sb.tile([P, M], F32, name="v2")
-        nc.vector.scalar_tensor_tensor(v2[:], h0p_sq[:], 1.0, xds[:], ALU.subtract, ALU.mult)
+        xs_sum = mid.tile([P, G], F32, name="xs_sum", offset=0, align_bytes=64)
+        w = mid.tile([P, M], F32, name="w", offset=2048, align_bytes=64)
+        p2, wt, q, ds2, hd, xds, v1, v2 = (
+            sb.tile([P, M], F32, name=name) for name in ("p2", "wt", "q", "ds2", "hd", "xds", "v1", "v2")
+        )
+        p2_sum = sb.tile([P, G], F32, name="p2_sum")
+        q_sum = sb.tile([P, G], F32, name="q_sum")
+        fused = nc.vector.scalar_tensor_tensor
+        steps = (
+            lambda m, g: group_sum(xs_sum[:, g], xs[:, m]),
+            lambda m, g: centre(w[:, m], xs[:, m], xs_sum[:, g], neg_k),
+            lambda m, g: fused(p2[:, m], th[:, m], 1.0, c0[:, m], ALU.add, ALU.mult),
+            lambda m, g: fused(wt[:, m], th[:, m], 1.0, w[:, m], ALU.subtract, ALU.mult),
+            lambda m, g: group_sum(p2_sum[:, g], p2[:, m]),
+            lambda m, g: fused(q[:, m], wt[:, m], quarter_gain[:], p2[:, m], ALU.mult, ALU.mult),
+            lambda m, g: centre(ds2[:, m], p2[:, m], p2_sum[:, g], neg_k),
+            lambda m, g: group_sum(q_sum[:, g], q[:, m]),
+            lambda m, g: fused(hd[:, m], ds2[:, m], -1.0, h0p[:, m], ALU.mult, ALU.mult),
+            lambda m, g: centre(xds[:, m], q[:, m], q_sum[:, g], neg_k),
+            lambda m, g: nc.vector.tensor_tensor(v1[:, m], hd[:, m], xs[:, m], ALU.mult),
+            lambda m, g: fused(v2[:, m], h0p_sq[:, m], 1.0, xds[:, m], ALU.subtract, ALU.mult),
+        )
+        for step in steps:
+            for h in range(2):
+                step(slice(h * M // 2, (h + 1) * M // 2), slice(h * G // 2, (h + 1) * G // 2))
         nc.vector.tensor_tensor(placed[:].indirect(offs2_t[:]), v1[:], v2[:], ALU.add)
 
         y = sb.tile([P, J], F32, name="y")
         for h, queue in enumerate((nc.sync, nc.scalar)):
             cols = slice(h * HALF, (h + 1) * HALF)
-            nc.vector.tensor_tensor(y[:, cols], placed[:, cols], base_t[:, cols], ALU.add)
+            nc.vector.scalar_tensor_tensor(y[:, cols], placed[:, cols], og_t, base_t[:, cols], ALU.mult, ALU.add)
             queue.dma_start(out=out[:, cols], in_=y[:, cols])

from contextlib import ExitStack

import concourse.mybir as mybir

K, R, F, T, J, M, G = 512, 128, 512, 2048, 512, 256, 32
FLOPS = 2 * K * R * J * 2 + 2 * F * R * M

F32 = mybir.dt.float32
BF16 = mybir.dt.bfloat16
I32 = mybir.dt.int32
U32 = mybir.dt.uint32
U16 = mybir.dt.uint16
U8 = mybir.dt.uint8
FP8X4 = mybir.dt.float8_e4m3fn_x4
ALU = mybir.AluOpType
ACT = mybir.ActivationFunctionType
AX = mybir.AxisListType

P = 128
PACK = 4
QUAD = 32
GROUP = M // G
HALF = J // 2
LIST_HALF = HALF // 16
DTAB_ROW = 4
TINY = 1e-30


def tile_attend_hvcpickcentred_kernel(
    tc, tab_words, tab_scales, w1, gain, share, pb, wo, dy, dtab_words, dtab_scales, og, base, offs, offs2, out
):
    nc = tc.nc
    with ExitStack() as ctx:
        sb = ctx.enter_context(tc.tile_pool(name="sb", bufs=1))
        shared = ctx.enter_context(tc.tile_pool(name="shared", bufs=1))
        mid = ctx.enter_context(tc.tile_pool(name="mid", bufs=1))
        ps = ctx.enter_context(tc.psum_pool(name="ps", bufs=1))

        def grouped(t):
            return t.rearrange("p (g e) -> p g e", e=GROUP)

        def group_sum(total, x):
            nc.vector.tensor_reduce(out=total, in_=grouped(x), axis=AX.X, op=ALU.add)

        def centre(res, x, total, neg_k):
            nc.vector.scalar_tensor_tensor(
                out=grouped(res),
                in0=total.unsqueeze(2).to_broadcast([P, total.shape[1], GROUP]),
                scalar=neg_k[:],
                in1=grouped(x),
                op0=ALU.mult,
                op1=ALU.add,
            )

        offs_t = sb.tile([P, J // 16], U16, name="offs_t")
        offs2_t = sb.tile([P, M // 16], U16, name="offs2_t")
        tab_s = sb.tile([P, T], U8, name="tab_s", tag="tab_scales_then_picked", align_bytes=64)
        dtab_s = sb.tile([P, T], U8, name="dtab_s", tag="dtab_scales_then_picked", align_bytes=64)
        w1_raw = shared.tile([P, PACK, R], F32, name="w1_raw", offset=7168, align_bytes=64)
        placed = sb.tile([P, J], F32, name="placed")
        ident = sb.tile([P, P], F32, name="ident")

        ones = sb.tile([P, QUAD], F32, name="ones", tag="tab_then_dtab_gs", align_bytes=64)
        col_count = sb.tile([P, QUAD], F32, name="col_count", align_bytes=64)
        row_count = sb.tile([P, QUAD], F32, name="row_count", align_bytes=64)
        nc.vector.memset(ones[:], 1.0)
        nc.vector.memset(tab_s[:].bitcast(I32), 0)
        nc.vector.tensor_tensor_scan(col_count[:], ones[:], ones[:], 0.0, ALU.mult, ALU.add)
        nc.vector.memset(dtab_s[:].bitcast(I32), 0)
        nc.vector.transpose(row_count[:], col_count[:])
        nc.vector.memset(ident[:], 0.0)
        for q0 in range(0, P, QUAD):
            rows = slice(q0, q0 + QUAD)
            nc.vector.tensor_tensor(ident[rows, rows], col_count[rows, :], row_count[rows, :], ALU.is_equal)
        nc.vector.memset(placed[:], 0.0)

        nc.sync.dma_start(out=w1_raw[:], in_=w1.rearrange("(p j) r -> p j r", j=PACK))
        nc.sync.dma_start(offs_t[:], offs)
        nc.sync.dma_start(offs2_t[:], offs2)
        for i, queue in enumerate((nc.sync, nc.scalar, nc.sync, nc.scalar)):
            queue.dma_start(out=tab_s[i:P:32, :].bitcast(I32), in_=tab_scales[0, i:16:4, :].bitcast(I32))
        tab_w = sb.tile([P, T], U32, name="tab_w", tag="tab_then_dtab_gs", align_bytes=64)
        nc.sync.dma_start(out=tab_w[:].bitcast(I32), in_=tab_words[0].rearrange("p n t -> p (n t)").bitcast(I32))
        for i in range(4):
            nc.sync.dma_start(
                out=dtab_s[DTAB_ROW + i : P : 32, :].bitcast(I32), in_=dtab_scales[0, i:16:4, :].bitcast(I32)
            )

        def interleave(inter, raw):
            nc.scalar.activation(out=inter[:], in_=raw[:].rearrange("p j w -> p w j"), func=ACT.Copy)

        def quantise(name, inter, width):
            codes = sb.tile([P, width], U32, name=name + "_codes", align_bytes=64)
            scales = sb.tile([P, width], U8, name=name + "_scales", align_bytes=64)
            nc.vector.quantize_mx(
                out=codes[:].bitcast(FP8X4), scales=scales[:], in_=inter[:].rearrange("p w j -> p (w j)")
            )
            return codes, scales

        w1_inter = shared.tile([P, R, PACK], BF16, name="w1_inter", offset=10368 + 4096 - 512, align_bytes=64)
        nc.vector.tensor_copy(out=w1_inter[:], in_=w1_raw[:].rearrange("p j w -> p w j"))

        dtab_w = shared.tile([P, T], U32, name="dtab_w", offset=0, align_bytes=64)
        vectors = shared.tile([P, 4, 8], F32, name="vectors", offset=8192, align_bytes=64)
        gain_t, share_t, og_t = vectors[:, 0, 0:1], vectors[:, 1, 0:1], vectors[:, 2, 0:1]
        pb_t = vectors[:, 3, 0:2]
        nc.sync.dma_start(out=gain_t, in_=gain)
        nc.sync.dma_start(out=pb_t, in_=pb.rearrange("o (p c) -> (o p) c", c=2))
        nc.sync.dma_start(out=dtab_w[:].bitcast(I32), in_=dtab_words[0].rearrange("p n t -> p (n t)").bitcast(I32))
        nc.sync.dma_start(out=share_t, in_=share)
        nc.sync.dma_start(out=og_t, in_=og)

        neg_gain = sb.tile([P, 1], F32, name="neg_gain")
        quarter_gain = sb.tile([P, 1], F32, name="quarter_gain")
        is_tiny = sb.tile([P, 1], F32, name="is_tiny")
        safe_gain = sb.tile([P, 1], F32, name="safe_gain")
        inv_gain = sb.tile([P, 1], F32, name="inv_gain")
        minus_one = sb.tile([P, 1], F32, name="minus_one")
        nc.scalar.activation(out=neg_gain[:], in_=gain_t, func=ACT.Copy, scale=-1.0)
        nc.scalar.activation(out=quarter_gain[:], in_=gain_t, func=ACT.Copy, scale=0.25)
        nc.vector.memset(minus_one[:], -1.0)
        nc.gpsimd.tensor_scalar(is_tiny[:], gain_t, gain_t, TINY, ALU.mult, ALU.is_lt)
        nc.gpsimd.tensor_scalar(safe_gain[:], gain_t, is_tiny[:], 1.0, ALU.add, ALU.mult)
        nc.gpsimd.tensor_tensor(inv_gain[:], safe_gain[:], minus_one[:], ALU.pow)

        tab_gs = sb.tile([P, J], U8, name="tab_gs", tag="tab_gs_then_base", align_bytes=64)
        nc.vector.tensor_copy(tab_gs[:], tab_s[:].indirect(offs_t[:]))
        w1_codes, w1_scales = quantise("w1", w1_inter, R)
        dy_raw = shared.tile([P, PACK, M], F32, name="dy_raw", offset=10368, align_bytes=64)
        wo_raw = shared.tile([P, PACK, R], F32, name="wo_raw", offset=10368 + 4096, align_bytes=64)
        nc.sync.dma_start(out=dy_raw[:], in_=dy.rearrange("(p j) m -> p j m", j=PACK))
        nc.sync.dma_start(out=wo_raw[:], in_=wo.rearrange("(p j) r -> p j r", j=PACK))

        def gather_and_multiply(name, words, scales, row, tag, sums):
            picked = sb.tile([P, J], U32, name=name + "_picked", tag=tag, align_bytes=64)
            for h in range(2):
                cols = slice(h * HALF, (h + 1) * HALF)
                nc.vector.tensor_copy(
                    picked[:, cols], words[:].indirect(offs_t[:, h * LIST_HALF : (h + 1) * LIST_HALF])
                )
                nc.tensor.matmul_mx(
                    out=sums[h],
                    lhsT=w1_codes[:].bitcast(FP8X4),
                    lhsT_scale=w1_scales[:],
                    rhs=picked[:, cols].bitcast(FP8X4),
                    rhs_scale=scales[row:P, cols],
                    start=True,
                    stop=True,
                )

        a_lo = ps.tile([P, HALF], F32, name="a_lo", tag="a_lo_then_pb")
        a_hi = ps.tile([P, HALF], F32, name="a_hi")
        a_ps = (a_lo[:], a_hi[:])
        gather_and_multiply("tab", tab_w, tab_gs, 0, "tab_scales_then_picked", a_ps)
        base_t = sb.tile([P, J], F32, name="base_t", tag="tab_gs_then_base", align_bytes=64)
        nc.sync.dma_start(out=base_t[:], in_=base)
        dtab_gs = sb.tile([P, J], U8, name="dtab_gs", tag="tab_then_dtab_gs", align_bytes=64)
        nc.vector.tensor_copy(dtab_gs[:], dtab_s[:].indirect(offs_t[:]))
        h0 = sb.tile([P, J], F32, name="h0")
        h1 = sb.tile([P, J], F32, name="h1")
        for h in range(2):
            cols = slice(h * HALF, (h + 1) * HALF)
            nc.scalar.activation(out=h0[:, cols], in_=a_ps[h], func=ACT.Tanh)
            nc.scalar.activation(out=h1[:, cols], in_=h0[:, cols], func=ACT.Copy, scale=gain_t)
        pb_ta = ps.tile([P, M + HALF], F32, name="pb_ta", tag="a_lo_then_pb")
        pb_ps = pb_ta[:, 0:M].rearrange("p (c n) -> p c n", c=2)
        for c in range(2):
            nc.tensor.transpose(pb_ps[:, c, :], pb_t[:, c : c + 1].to_broadcast([P, P]), ident[:])

        h0_sq = mid.tile([P, J], F32, name="h0_sq", offset=1088, align_bytes=64)
        slope = sb.tile([P, J], F32, name="slope")
        nc.scalar.activation(out=h0_sq[:], in_=h0[:], func=ACT.Square)
        nc.scalar.activation(out=slope[:], in_=h0_sq[:], func=ACT.Identity, scale=neg_gain[:], bias=gain_t)

        neg_k = mid.tile([P, 1], F32, name="neg_k", offset=3072, align_bytes=64)
        nc.scalar.activation(out=neg_k[:], in_=share_t, func=ACT.Copy, scale=-1.0 / GROUP)
        dy_inter = mid.tile([P, M, PACK], BF16, name="dy_inter", offset=0, align_bytes=64)
        wo_inter = mid.tile([P, R, PACK], BF16, name="wo_inter", offset=2048, align_bytes=64)
        interleave(dy_inter, dy_raw)
        interleave(wo_inter, wo_raw)

        ta_hi = ps.tile([P, HALF], F32, name="ta_hi")
        ta_ps = (pb_ta[:, M : M + HALF], ta_hi[:])
        gather_and_multiply("dtab", dtab_w, dtab_gs, DTAB_ROW, "dtab_scales_then_picked", ta_ps)

        hp = shared.tile([P, M], F32, name="hp", offset=0, align_bytes=64)
        nc.vector.tensor_copy(hp[:], h1[:].indirect(offs2_t[:]))

        xh1 = sb.tile([P, J], F32, name="xh1")
        s = sb.tile([P, M], F32, name="s")
        nc.vector.tensor_tensor(xh1[:, 0:HALF], ta_ps[0], slope[:, 0:HALF], ALU.mult)
        nc.vector.tensor_tensor(
            s[:].rearrange("p (n c) -> p n c", c=2),
            hp[:].rearrange("p (n c) -> p n c", c=2),
            pb_ps.rearrange("p c n -> p n c"),
            ALU.add,
        )
        nc.vector.tensor_tensor(xh1[:, HALF:J], ta_ps[1], slope[:, HALF:J], ALU.mult)
        s_sum = sb.tile([P, G], F32, name="s_sum")
        group_sum(s_sum[:], s[:])
        xs = sb.tile([P, M], F32, name="xs")
        nc.vector.tensor_copy(xs[:], xh1[:].indirect(offs2_t[:]))
        u = sb.tile([P, M], F32, name="u")
        centre(u[:], s[:], s_sum[:], neg_k)
        th = shared.tile([P, M], F32, name="th", offset=10368 + 4096 + 512, align_bytes=64)
        nc.scalar.activation(out=th[:], in_=u[:], func=ACT.Tanh, scale=0.5)
        h0p_sq = shared.tile([P, M], F32, name="h0p_sq", offset=10368 + 4096 + 1536, align_bytes=64)
        h0p = shared.tile([P, M], F32, name="h0p", offset=10368 + 4096 - 512, align_bytes=64)
        nc.scalar.activation(out=h0p[:], in_=hp[:], func=ACT.Copy, scale=inv_gain[:])
        nc.scalar.activation(out=h0p_sq[:], in_=hp[:], func=ACT.Square, scale=inv_gain[:])

        dy_codes, dy_scales = quantise("dy", dy_inter, M)
        wo_codes, wo_scales = quantise("wo", wo_inter, R)
        c0 = ps.tile([P, M], F32, name="c0")
        nc.tensor.matmul_mx(
            out=c0[:],
            lhsT=wo_codes[:].bitcast(FP8X4),
            lhsT_scale=wo_scales[:],
            rhs=dy_codes[:].bitcast(FP8X4),
            rhs_scale=dy_scales[:],
            start=True,
            stop=True,
        )

        xs_sum = mid.tile([P, G], F32, name="xs_sum", offset=0, align_bytes=64)
        w = mid.tile([P, M], F32, name="w", offset=2048, align_bytes=64)
        p2, wt, q, ds2, hd, xds, v1, v2 = (
            sb.tile([P, M], F32, name=name) for name in ("p2", "wt", "q", "ds2", "hd", "xds", "v1", "v2")
        )
        p2_sum = sb.tile([P, G], F32, name="p2_sum")
        q_sum = sb.tile([P, G], F32, name="q_sum")
        fused = nc.vector.scalar_tensor_tensor
        steps = (
            lambda m, g: group_sum(xs_sum[:, g], xs[:, m]),
            lambda m, g: centre(w[:, m], xs[:, m], xs_sum[:, g], neg_k),
            lambda m, g: fused(p2[:, m], th[:, m], 1.0, c0[:, m], ALU.add, ALU.mult),
            lambda m, g: fused(wt[:, m], th[:, m], 1.0, w[:, m], ALU.subtract, ALU.mult),
            lambda m, g: group_sum(p2_sum[:, g], p2[:, m]),
            lambda m, g: fused(q[:, m], wt[:, m], quarter_gain[:], p2[:, m], ALU.mult, ALU.mult),
            lambda m, g: centre(ds2[:, m], p2[:, m], p2_sum[:, g], neg_k),
            lambda m, g: group_sum(q_sum[:, g], q[:, m]),
            lambda m, g: fused(hd[:, m], ds2[:, m], -1.0, h0p[:, m], ALU.mult, ALU.mult),
            lambda m, g: centre(xds[:, m], q[:, m], q_sum[:, g], neg_k),
            lambda m, g: nc.vector.tensor_tensor(v1[:, m], hd[:, m], xs[:, m], ALU.mult),
            lambda m, g: fused(v2[:, m], h0p_sq[:, m], 1.0, xds[:, m], ALU.subtract, ALU.mult),
        )
        for step in steps:
            for h in range(2):
                step(slice(h * M // 2, (h + 1) * M // 2), slice(h * G // 2, (h + 1) * G // 2))
        nc.vector.tensor_tensor(placed[:].indirect(offs2_t[:]), v1[:], v2[:], ALU.add)

        y = sb.tile([P, J], F32, name="y")
        for h, queue in enumerate((nc.sync, nc.scalar)):
            cols = slice(h * HALF, (h + 1) * HALF)
            nc.vector.scalar_tensor_tensor(y[:, cols], placed[:, cols], og_t, base_t[:, cols], ALU.mult, ALU.add)
            queue.dma_start(out=out[:, cols], in_=y[:, cols])
